import numpy as np
import ml_dtypes


def mxq(x, axis, fmt="e4m3"):
    dtype, down = {"e4m3": (ml_dtypes.float8_e4m3fn, 7), "e5m2": (ml_dtypes.float8_e5m2, 14)}[fmt]
    v = np.moveaxis(np.asarray(x, np.float32).astype(ml_dtypes.bfloat16).astype(np.float64), axis, -1)
    blocks = v.reshape(v.shape[:-1] + (-1, 32))
    amax = np.abs(blocks).max(-1, keepdims=True)
    byte = np.maximum(np.where(amax > 0, np.frexp(amax)[1] - 1 + 127, 0) - down, 1)
    scale = np.exp2(byte - 127.0)
    codes = (blocks / scale).astype(np.float32).astype(dtype).astype(np.float64)
    return np.moveaxis((codes * scale).reshape(v.shape), -1, axis)


WIDE = False


def mx_kscale(k):
    if not WIDE:
        return np.ones(k)
    levels = np.array([10, -10, 5, -5, 0])
    if k % 512:
        return np.exp2(np.random.permutation(np.resize(levels, k // 32))).repeat(32)
    a = np.empty((k // 512, 16))
    for p in range(k // 512):
        a[p, :8] = np.random.permutation(np.resize(levels, 8))
        for g in range(8):
            far = levels[np.abs(levels - a[p, g]) >= 10]
            a[p, g + 8] = far[np.random.randint(len(far))]
    return np.exp2(a.ravel()).repeat(32)


def f64(x):
    return np.asarray(x).astype(np.float64)


def striped(idx):
    return np.tile(np.asarray(idx).reshape(-1, 16).T, (8, 1)).astype(np.uint16)


def unstriped(offs):
    return offs[:16].T.reshape(-1).astype(np.int64)


def striped8(idx):
    return np.asarray(idx).reshape(8, -1, 16).transpose(0, 2, 1).reshape(128, -1).astype(np.uint16)


def unstriped8(offs):
    return offs.reshape(8, 16, -1).transpose(0, 2, 1).reshape(8, -1).astype(np.int64)


def pick8(x, idx, run):
    r = np.arange(len(x))
    return x[r[:, None], idx[r % (8 * run) // run]]


E2M1 = np.array([0.0, 0.5, 1.0, 1.5, 2.0, 3.0, 4.0, 6.0, -0.0, -0.5, -1.0, -1.5, -2.0, -3.0, -4.0, -6.0])


def pack_weight(w, fmt):
    k, n = w.shape
    w = f64(np.asarray(w, np.float32).astype(ml_dtypes.bfloat16)).reshape(k // 32, 32, n)
    amax = np.abs(w).max(1)
    if fmt == "e4m3":
        byte = np.frexp(amax)[1] - 1 + 127 - 7
    else:
        mant, ex = np.frexp(amax / 6.0)
        byte = np.where(mant > 0.5, ex, ex - 1) + 127
    byte = np.clip(np.where(amax > 0, byte, 1), 1, 254)
    scaled = (w * np.exp2(127.0 - byte)[:, None, :]).reshape(k, n).astype(np.float32)
    by_word = np.ascontiguousarray(scaled.reshape(k // 512, 128, 4, n).transpose(0, 1, 3, 2))
    if fmt == "e4m3":
        words = by_word.astype(ml_dtypes.float8_e4m3fn).view(np.uint8)
    else:
        c = by_word.astype(ml_dtypes.float4_e2m1fn).view(np.uint8) & 0xF
        words = (c[..., 0::2] | (c[..., 1::2] << 4)).reshape(k // 512, 128, 2 * n)
    return np.ascontiguousarray(words), np.ascontiguousarray(byte.astype(np.uint8).reshape(k // 512, 16, n))


def unpack_weight(words, scales, fmt):
    g, _, n = scales.shape
    words = np.ascontiguousarray(words).reshape(g, 128, n, -1)
    if fmt == "e4m3":
        vals = words.view(ml_dtypes.float8_e4m3fn).astype(np.float64)
    else:
        nib = np.empty((g, 128, n, 4), np.uint8)
        nib[..., 0::2] = words & 0xF
        nib[..., 1::2] = words >> 4
        vals = E2M1[nib]
    vals = vals * np.repeat(np.exp2(scales.astype(np.float64) - 127.0), 8, axis=1)[..., None]
    return vals.transpose(0, 1, 3, 2).reshape(g * 512, n)


K, J, R, T, C, N, S, U = 512, 384, 512, 1024, 512, 256, 1024, 1024


def setup_inputs():
    n = np.random.standard_normal
    idx = np.random.permutation(T)[:J]
    idx2 = np.stack([np.random.permutation(C)[:J] for _ in range(8)])
    idx3 = np.stack([np.random.permutation(C)[:J] for _ in range(8)])
    idx4 = np.random.permutation(S)[:N]
    idx5 = np.stack([np.random.permutation(U)[:C] for _ in range(8)])
    idx6 = np.stack([np.random.permutation(U)[:C] for _ in range(8)])
    fk = mx_kscale(K)
    fr = mx_kscale(R)
    xtp = pack_weight(n((K, T)) * fk[:, None], "e2m1")
    wp = pack_weight(n((K, R)) * 1 / np.sqrt(K) / fk[:, None] * fr, "e4m3")
    w2p = pack_weight(n((K, R)) * 1 / np.sqrt(K) / fk[:, None] * fr, "e4m3")
    vsp = pack_weight(n((R, S)) * 1 / np.sqrt(R) / fr[:, None], "e2m1")
    return {
        "xt_words": xtp[0],
        "xt_scales": xtp[1],
        "w_words": wp[0],
        "w_scales": wp[1],
        "w2_words": w2p[0],
        "w2_scales": w2p[1],
        "vs_words": vsp[0],
        "vs_scales": vsp[1],
        "offs": striped(idx),
        "offs2": striped8(idx2),
        "offs3": striped8(idx3),
        "offs4": striped(idx4),
        "offs5": striped8(idx5),
        "offs6": striped8(idx6),
    }


def reference(xt_words, xt_scales, w_words, w_scales, w2_words, w2_scales, vs_words, vs_scales, offs, offs2, offs3, offs4, offs5, offs6):
    idx = unstriped(offs)
    idx2 = unstriped8(offs2)
    idx3 = unstriped8(offs3)
    idx4 = unstriped(offs4)
    idx5 = unstriped8(offs5)
    idx6 = unstriped8(offs6)
    xtu = unpack_weight(xt_words, xt_scales, "e2m1")
    wu = unpack_weight(w_words, w_scales, "e4m3")
    w2u = unpack_weight(w2_words, w2_scales, "e4m3")
    vsu = unpack_weight(vs_words, vs_scales, "e2m1")
    xtidxg = xtu[:, idx]
    a = wu.T @ xtidxg
    b = w2u.T @ xtidxg
    pw = np.zeros((R, C))
    pw[np.arange(R)[:, None], idx2[np.arange(R) % 512 // 64]] = a
    pv = np.zeros((R, C))
    pv[np.arange(R)[:, None], idx3[np.arange(R) % 512 // 64]] = b
    hid = np.minimum(np.abs(pw), np.abs(pv))
    vsidx4g = vsu[:, idx4]
    hidq = mxq(hid, 0, "e4m3")
    p = vsidx4g.T @ hidq
    m0 = np.zeros((N, U))
    m0[np.arange(N)[:, None], idx5[np.arange(N) % 128 // 16]] = p
    m1 = np.zeros((N, U))
    m1[np.arange(N)[:, None], idx6[np.arange(N) % 128 // 16]] = p
    y = m0 - m1
    return y

@@ -1,0 +1,237 @@
+from contextlib import ExitStack
+
+import concourse.mybir as mybir
+
+K, J, R, T, C, N, S, U = 512, 384, 512, 1024, 512, 256, 1024, 1024
+FLOPS = 2 * (2 * K * R * J + R * N * C)
+
+F32 = mybir.dt.float32
+BF16 = mybir.dt.bfloat16
+I32 = mybir.dt.int32
+U32 = mybir.dt.uint32
+U16 = mybir.dt.uint16
+U8 = mybir.dt.uint8
+FP8X4 = mybir.dt.float8_e4m3fn_x4
+FP4X4 = mybir.dt.float4_e2m1fn_x4
+ALU = mybir.AluOpType
+COPY = mybir.ActivationFunctionType.Copy
+
+P = 128
+PACK = 4
+QUADS = 4
+STRIPE = 16
+SLOT_PIECES = ((0, 128), (128, J))
+COLUMN_PIECES = ((0, 128), (128, 256), (256, C))
+STORE_PIECES = ((0, 256), (256, 512), (512, 768), (768, U))
+
+
+def tile_picked_tokens_plain_twin_bothlanded_store_divergence_kernel(
+    tc, xt_words, xt_scales, w_words, w_scales, w2_words, w2_scales, vs_words, vs_scales,
+    offs, offs2, offs3, offs4, offs5, offs6, out,
+):
+    nc = tc.nc
+    with ExitStack() as ctx:
+        lists = ctx.enter_context(tc.tile_pool(name="lists", bufs=1))
+        sb = ctx.enter_context(tc.tile_pool(name="sb", bufs=1))
+        ps = ctx.enter_context(tc.psum_pool(name="ps", bufs=1))
+
+        def load_list(src, name):
+            held = lists.tile(list(src.shape), U16, name=name)
+            nc.sync.dma_start(held[:], src)
+            return held
+
+        def entries(held, lo, hi):
+            return held[:, lo // STRIPE : hi // STRIPE]
+
+        def zeroed_plane(width, name):
+            plane = sb.tile([P, width], U8, name=name, align_bytes=64)
+            nc.vector.memset(plane[:].bitcast(I32), 0)
+            return plane
+
+        def load_scale_rows(scales, name):
+            width = scales.shape[2]
+            plane = sb.tile([P, width], U8, name=name, align_bytes=64)
+            for q in range(QUADS):
+                rows = scales[0, 4 * q : 4 * q + 4, :].bitcast(I32)
+                nc.sync.dma_start(
+                    plane[32 * q : 32 * q + 32, :].bitcast(I32),
+                    rows.unsqueeze(0).broadcast_to([8, 4, width // 4]),
+                )
+            return plane
+
+        def zeroed_board(width, name, tag):
+            board = sb.tile([P, width], F32, name=name, tag=tag, align_bytes=64)
+            nc.vector.memset(board[:], 0.0)
+            return board
+
+        def deal_scales(plane, t0, t1, name):
+            dealt = sb.tile([P, t1 - t0, P], U8, name=name, align_bytes=64)
+            nc.vector.tensor_copy(dealt[:], plane[:].rearrange("p (m t) -> p t m", t=PACK)[:, t0:t1, :])
+            return dealt
+
+        def scatter(board, held, lo, hi, values):
+            nc.scalar.activation(out=board[:].indirect(entries(held, lo, hi)), in_=values, func=COPY)
+
+        ws_plane = zeroed_plane(R, "ws_plane")
+        l1 = load_list(offs, "l1")
+        xw_win = sb.tile([P, T], U16, name="xw_win", align_bytes=64)
+        xs_win = load_scale_rows(xt_scales, "xs_win")
+        ws_stage = sb.tile([4, QUADS, R // 4], I32, name="ws_stage")
+        nc.scalar.dma_start(ws_stage[:], w_scales[0].bitcast(I32).rearrange("(q i) c -> i q c", i=4))
+        nc.scalar.dma_start(xw_win[:].bitcast(I32), xt_words[0].bitcast(I32))
+        w_raw = sb.tile([P, R], U32, name="w_raw", align_bytes=64)
+        nc.scalar.dma_start(w_raw[:].bitcast(I32), w_words[0].rearrange("p n t -> p (n t)").bitcast(I32))
+        l2 = load_list(offs2, "l2")
+        w2_raw = sb.tile([P, R], I32, name="w2_raw", align_bytes=64)
+        nc.sync.dma_start(w2_raw[:], w2_words[0].rearrange("p n t -> p (n t)").bitcast(I32))
+        w2s_plane = load_scale_rows(w2_scales, "w2s_plane")
+        l3 = load_list(offs3, "l3")
+        vw_win = sb.tile([P, S], U16, name="vw_win", align_bytes=64)
+        nc.sync.dma_start(vw_win[:].bitcast(I32), vs_words[0].bitcast(I32))
+        vss_win = load_scale_rows(vs_scales, "vss_win")
+        l4 = load_list(offs4, "l4")
+        l5 = load_list(offs5, "l5")
+        l6 = load_list(offs6, "l6")
+        pw = [zeroed_board(C, "pw%d" % i, "pw%d" % i) for i in range(2)]
+        pv = [zeroed_board(C, "pv%d" % i, "pv%d" % i) for i in range(2)]
+        plus = [zeroed_board(U, "plus0", "plus0")]
+
+        for q in range(QUADS):
+            nc.vector.tensor_copy(ws_plane[32 * q : 32 * q + 4, :].bitcast(I32), ws_stage[:, q, :])
+        ws_dealt = [deal_scales(ws_plane, 0, 2, "ws_dealt0")]
+        w_dealt = []
+        for h in range(2):
+            dealt = sb.tile([P, 2, P], U32, name="w_dealt%d" % h, align_bytes=64)
+            nc.scalar.copy(
+                dealt[:].rearrange("p t m -> p m t"),
+                w_raw[:].rearrange("p (m t) -> p m t", t=PACK)[:, :, 2 * h : 2 * h + 2],
+            )
+            w_dealt.append(dealt)
+
+        xw = sb.tile([P, J], U16, name="xw", align_bytes=64)
+        xs = sb.tile([P, J], U8, name="xs", align_bytes=64)
+        for lo, hi in SLOT_PIECES:
+            nc.vector.tensor_copy(xw[:, lo:hi], xw_win[:].indirect(entries(l1, lo, hi)))
+            nc.vector.tensor_copy(xs[:, lo:hi], xs_win[:].indirect(entries(l1, lo, hi)))
+
+        def first_product(acc, words, scales, lo, hi):
+            nc.tensor.matmul_mx(
+                out=acc, lhsT=words.bitcast(FP8X4), lhsT_scale=scales,
+                rhs=xw[:, lo:hi].bitcast(FP4X4), rhs_scale=xs[:, lo:hi], start=True, stop=True,
+            )
+
+        a_vals = [sb.tile([P, J], F32, name="a_vals%d" % t) for t in range(PACK)]
+        for lo, hi in SLOT_PIECES:
+            for t in range(2):
+                acc = ps.tile([P, hi - lo], F32, name="piece", tag="piece", bufs=4)
+                first_product(acc[:], w_dealt[0][:, t, :], ws_dealt[0][:, t, :], lo, hi)
+                if lo == 0 and t == 0:
+                    nc.scalar.activation(out=a_vals[t][:, lo:hi], in_=acc[:], func=COPY)
+                else:
+                    nc.vector.tensor_copy(a_vals[t][:, lo:hi], acc[:])
+                scatter(pw[t], l2, lo, hi, a_vals[t][:, lo:hi])
+
+        w2_dealt = sb.tile([P, PACK, P], I32, name="w2_dealt", align_bytes=64)
+        nc.vector.tensor_copy(
+            w2_dealt[:].rearrange("p t m -> p m t"), w2_raw[:].rearrange("p (m t) -> p m t", t=PACK)
+        )
+        w2s_dealt = deal_scales(w2s_plane, 0, PACK, "w2s_dealt")
+        ws_dealt.append(deal_scales(ws_plane, 2, PACK, "ws_dealt1"))
+
+        def whole_product(words, scales):
+            acc = ps.tile([P, J], F32, name="whole", tag="whole", bufs=3)
+            for lo, hi in SLOT_PIECES:
+                first_product(acc[:, lo:hi], words, scales, lo, hi)
+            return acc
+
+        def magnitude(dst, src):
+            nc.vector.scalar_tensor_tensor(out=dst, in0=src, scalar=-1.0, in1=src, op0=ALU.mult, op1=ALU.max)
+
+        def land_a(t):
+            acc = whole_product(w_dealt[1][:, t - 2, :], ws_dealt[1][:, t - 2, :])
+            nc.vector.tensor_copy(a_vals[t][:], acc[:])
+            scatter(pw[t % 2], l2, 0, J, a_vals[t][:])
+
+        def land_b(t):
+            acc = whole_product(w2_dealt[:, t, :], w2s_dealt[:, t, :])
+            b_vals = sb.tile([P, J], F32, name="b_vals%d" % t, tag="after_b%d" % t, align_bytes=64)
+            nc.vector.tensor_copy(b_vals[:], acc[:])
+            b_mag = sb.tile([P, J], F32, name="b_mag%d" % t)
+            magnitude(b_mag[:], b_vals[:])
+            scatter(pv[t % 2], l3, 0, J, b_mag[:])
+
+        pw_mag = [sb.tile([P, C], F32, name="pw_mag%d" % t) for t in range(PACK)]
+        hid_rows = sb.tile([P, PACK - 1, C], BF16, name="hid_rows", tag="reuse3", align_bytes=64)
+
+        def smaller(dst, t, lo, hi):
+            nc.vector.tensor_tensor(dst, pw_mag[t][:, lo:hi], pv[t % 2][:, lo:hi], ALU.min)
+
+        land_b(0)
+        land_b(1)
+        magnitude(pw_mag[0][:], pw[0][:])
+        magnitude(pw_mag[1][:], pw[1][:])
+        land_a(2)
+        smaller(hid_rows[:, 0, :], 0, 0, C)
+        land_b(2)
+        land_a(3)
+        smaller(hid_rows[:, 1, :], 1, 0, C)
+        land_b(3)
+
+        vw = sb.tile([P, N], U16, name="vw", tag="after_b0", align_bytes=64)
+        vsc = sb.tile([P, N], U8, name="vsc", tag="after_b1", align_bytes=64)
+        nc.vector.tensor_copy(vw[:], vw_win[:].indirect(l4[:]))
+        nc.vector.tensor_copy(vsc[:], vss_win[:].indirect(l4[:]))
+        minus = zeroed_board(U, "minus", "after_b2")
+
+        magnitude(pw_mag[2][:], pw[0][:])
+        smaller(hid_rows[:, 2, :], 2, 0, C)
+
+        def weave(lo, hi):
+            woven = sb.tile([P, hi - lo, PACK], BF16, name="hid", tag="hid", bufs=2, align_bytes=64)
+            nc.vector.tensor_copy(
+                woven[:, :, 0 : PACK - 1], hid_rows[:, :, lo:hi].rearrange("p t c -> p c t")
+            )
+            return woven
+
+        hid = [weave(lo, hi) for lo, hi in COLUMN_PIECES[:2]]
+        magnitude(pw_mag[3][:], pw[1][:])
+
+        p_vals = [sb.tile([P, C], F32, name="p_vals%d" % nt) for nt in range(2)]
+        acc1 = ps.tile([P, C], F32, name="acc1", tag="acc1", bufs=1)
+
+        def second_product(acc, nt, codes, scales):
+            nc.tensor.matmul_mx(
+                out=acc, lhsT=vw[:, nt * P : (nt + 1) * P].bitcast(FP4X4), lhsT_scale=vsc[:, nt * P : (nt + 1) * P],
+                rhs=codes[:].bitcast(FP8X4), rhs_scale=scales[:], start=True, stop=True,
+            )
+
+        for i, (lo, hi) in enumerate(COLUMN_PIECES):
+            if i == len(hid):
+                hid.append(weave(lo, hi))
+            smaller(hid[i][:, :, PACK - 1], PACK - 1, lo, hi)
+            codes = sb.tile([P, hi - lo], U32, name="codes%d" % i, align_bytes=64)
+            scales = sb.tile([P, hi - lo], U8, name="scales%d" % i, align_bytes=64)
+            nc.vector.quantize_mx(
+                out=codes[:].bitcast(FP8X4), scales=scales[:], in_=hid[i][:].rearrange("p c t -> p (c t)")
+            )
+            acc = ps.tile([P, hi - lo], F32, name="piece", tag="piece", bufs=4)
+            second_product(acc[:], 0, codes, scales)
+            second_product(acc1[:, lo:hi], 1, codes, scales)
+            if i == 0:
+                nc.scalar.copy(p_vals[0][:, lo:hi], acc[:])
+            else:
+                nc.vector.tensor_copy(p_vals[0][:, lo:hi], acc[:])
+            scatter(plus[0], l5, lo, hi, p_vals[0][:, lo:hi])
+            scatter(minus, l6, lo, hi, p_vals[0][:, lo:hi])
+        nc.vector.tensor_copy(p_vals[1][:], acc1[:])
+
+        plus.append(zeroed_board(U, "plus1", "reuse3"))
+        page0 = sb.tile([P, U], F32, name="page0")
+        nc.vector.tensor_tensor(page0[:], plus[0][:], minus[:], ALU.subtract)
+        nc.sync.dma_start(out[0:P, :], page0[:])
+        scatter(plus[1], l5, 0, C, p_vals[1][:])
+        scatter(minus, l6, 0, C, p_vals[1][:])
+        for i, (lo, hi) in enumerate(STORE_PIECES):
+            page = sb.tile([P, hi - lo], F32, name="page1_%d" % i)
+            nc.vector.tensor_tensor(page[:], plus[1][:, lo:hi], minus[:, lo:hi], ALU.subtract)
+            nc.sync.dma_start(out[P : 2 * P, lo:hi], page[:])

@@ -21,8 +21,8 @@ PACK = 4
 QUADS = 4
 STRIPE = 16
 SLOT_PIECES = ((0, 128), (128, J))
-COLUMN_PIECES = ((0, 128), (128, 256), (256, C))
-STORE_PIECES = ((0, 256), (256, 512), (512, 768), (768, U))
+COLUMN_PIECES = tuple((lo, lo + 128) for lo in range(0, C, 128))
+STORE_PIECES = ((0, 128), (128, 384), (384, 640), (640, 896), (896, U))
 
 
 def tile_picked_tokens_plain_twin_bothlanded_store_divergence_kernel(
@@ -79,7 +79,7 @@ def tile_picked_tokens_plain_twin_bothlanded_store_divergence_kernel(
         ws_stage = sb.tile([4, QUADS, R // 4], I32, name="ws_stage")
         nc.scalar.dma_start(ws_stage[:], w_scales[0].bitcast(I32).rearrange("(q i) c -> i q c", i=4))
         nc.scalar.dma_start(xw_win[:].bitcast(I32), xt_words[0].bitcast(I32))
-        w_raw = sb.tile([P, R], U32, name="w_raw", align_bytes=64)
+        w_raw = sb.tile([P, R], U32, name="w_raw", tag="after_w", align_bytes=64)
         nc.scalar.dma_start(w_raw[:].bitcast(I32), w_words[0].rearrange("p n t -> p (n t)").bitcast(I32))
         l2 = load_list(offs2, "l2")
         w2_raw = sb.tile([P, R], I32, name="w2_raw", align_bytes=64)
@@ -94,11 +94,10 @@ def tile_picked_tokens_plain_twin_bothlanded_store_divergence_kernel(
         l6 = load_list(offs6, "l6")
         pw = [zeroed_board(C, "pw%d" % i, "pw%d" % i) for i in range(2)]
         pv = [zeroed_board(C, "pv%d" % i, "pv%d" % i) for i in range(2)]
-        plus = [zeroed_board(U, "plus0", "plus0")]
 
         for q in range(QUADS):
             nc.vector.tensor_copy(ws_plane[32 * q : 32 * q + 4, :].bitcast(I32), ws_stage[:, q, :])
-        ws_dealt = [deal_scales(ws_plane, 0, 2, "ws_dealt0")]
+        ws_dealt = [deal_scales(ws_plane, t, t + 1, "ws_dealt%d" % t) for t in range(2)]
         w_dealt = []
         for h in range(2):
             dealt = sb.tile([P, 2, P], U32, name="w_dealt%d" % h, align_bytes=64)
@@ -108,23 +107,24 @@ def tile_picked_tokens_plain_twin_bothlanded_store_divergence_kernel(
             )
             w_dealt.append(dealt)
 
-        xw = sb.tile([P, J], U16, name="xw", align_bytes=64)
-        xs = sb.tile([P, J], U8, name="xs", align_bytes=64)
-        for lo, hi in SLOT_PIECES:
-            nc.vector.tensor_copy(xw[:, lo:hi], xw_win[:].indirect(entries(l1, lo, hi)))
-            nc.vector.tensor_copy(xs[:, lo:hi], xs_win[:].indirect(entries(l1, lo, hi)))
+        xw, xs = {}, {}
+        for (lo, hi), word_tag, scale_tag in zip(SLOT_PIECES, ("xw_first", "after_w"), ("xs_first", "xs_rest")):
+            xw[lo] = sb.tile([P, hi - lo], U16, name="xw%d" % lo, tag=word_tag, align_bytes=64)
+            xs[lo] = sb.tile([P, hi - lo], U8, name="xs%d" % lo, tag=scale_tag, align_bytes=64)
+            nc.vector.tensor_copy(xw[lo][:], xw_win[:].indirect(entries(l1, lo, hi)))
+            nc.vector.tensor_copy(xs[lo][:], xs_win[:].indirect(entries(l1, lo, hi)))
 
         def first_product(acc, words, scales, lo, hi):
             nc.tensor.matmul_mx(
                 out=acc, lhsT=words.bitcast(FP8X4), lhsT_scale=scales,
-                rhs=xw[:, lo:hi].bitcast(FP4X4), rhs_scale=xs[:, lo:hi], start=True, stop=True,
+                rhs=xw[lo][:].bitcast(FP4X4), rhs_scale=xs[lo][:], start=True, stop=True,
             )
 
         a_vals = [sb.tile([P, J], F32, name="a_vals%d" % t) for t in range(PACK)]
         for lo, hi in SLOT_PIECES:
             for t in range(2):
                 acc = ps.tile([P, hi - lo], F32, name="piece", tag="piece", bufs=4)
-                first_product(acc[:], w_dealt[0][:, t, :], ws_dealt[0][:, t, :], lo, hi)
+                first_product(acc[:], w_dealt[0][:, t, :], ws_dealt[t][:, 0, :], lo, hi)
                 if lo == 0 and t == 0:
                     nc.scalar.activation(out=a_vals[t][:, lo:hi], in_=acc[:], func=COPY)
                 else:
@@ -136,7 +136,7 @@ def tile_picked_tokens_plain_twin_bothlanded_store_divergence_kernel(
             w2_dealt[:].rearrange("p t m -> p m t"), w2_raw[:].rearrange("p (m t) -> p m t", t=PACK)
         )
         w2s_dealt = deal_scales(w2s_plane, 0, PACK, "w2s_dealt")
-        ws_dealt.append(deal_scales(ws_plane, 2, PACK, "ws_dealt1"))
+        ws_dealt.append(deal_scales(ws_plane, 2, PACK, "ws_dealt2"))
 
         def whole_product(words, scales):
             acc = ps.tile([P, J], F32, name="whole", tag="whole", bufs=3)
@@ -147,21 +147,34 @@ def tile_picked_tokens_plain_twin_bothlanded_store_divergence_kernel(
         def magnitude(dst, src):
             nc.vector.scalar_tensor_tensor(out=dst, in0=src, scalar=-1.0, in1=src, op0=ALU.mult, op1=ALU.max)
 
-        def land_a(t):
-            acc = whole_product(w_dealt[1][:, t - 2, :], ws_dealt[1][:, t - 2, :])
+        def make_a(t):
+            acc = whole_product(w_dealt[1][:, t - 2, :], ws_dealt[2][:, t - 2, :])
             nc.vector.tensor_copy(a_vals[t][:], acc[:])
-            scatter(pw[t % 2], l2, 0, J, a_vals[t][:])
 
-        def land_b(t):
+        def make_b(t):
             acc = whole_product(w2_dealt[:, t, :], w2s_dealt[:, t, :])
             b_vals = sb.tile([P, J], F32, name="b_vals%d" % t, tag="after_b%d" % t, align_bytes=64)
             nc.vector.tensor_copy(b_vals[:], acc[:])
             b_mag = sb.tile([P, J], F32, name="b_mag%d" % t)
             magnitude(b_mag[:], b_vals[:])
-            scatter(pv[t % 2], l3, 0, J, b_mag[:])
+            return b_mag
 
-        pw_mag = [sb.tile([P, C], F32, name="pw_mag%d" % t) for t in range(PACK)]
-        hid_rows = sb.tile([P, PACK - 1, C], BF16, name="hid_rows", tag="reuse3", align_bytes=64)
+        b_mags = [make_b(0), make_b(1)]
+        for t in (2, 3):
+            make_a(t)
+            b_mags.append(make_b(t))
+
+        def land_a(t):
+            scatter(pw[t % 2], l2, 0, J, a_vals[t][:])
+
+        def land_b(t):
+            scatter(pv[t % 2], l3, 0, J, b_mags[t][:])
+
+        pw_mag = [
+            sb.tile([P, C], F32, name="pw_mag%d" % t, tag="after_b%d" % t if t < 2 else "pw_mag%d" % t, align_bytes=64)
+            for t in range(PACK - 1)
+        ]
+        hid_rows = sb.tile([P, PACK - 1, C], BF16, name="hid_rows")
 
         def smaller(dst, t, lo, hi):
             nc.vector.tensor_tensor(dst, pw_mag[t][:, lo:hi], pv[t % 2][:, lo:hi], ALU.min)
@@ -177,24 +190,22 @@ def tile_picked_tokens_plain_twin_bothlanded_store_divergence_kernel(
         smaller(hid_rows[:, 1, :], 1, 0, C)
         land_b(3)
 
-        vw = sb.tile([P, N], U16, name="vw", tag="after_b0", align_bytes=64)
-        vsc = sb.tile([P, N], U8, name="vsc", tag="after_b1", align_bytes=64)
+        vw = sb.tile([P, N], U16, name="vw", tag="after_b2", align_bytes=64)
+        vsc = sb.tile([P, N], U8, name="vsc", tag="after_b3", align_bytes=64)
         nc.vector.tensor_copy(vw[:], vw_win[:].indirect(l4[:]))
         nc.vector.tensor_copy(vsc[:], vss_win[:].indirect(l4[:]))
-        minus = zeroed_board(U, "minus", "after_b2")
+        plus = [zeroed_board(U, "plus0", "xs_rest")]
+        minus = zeroed_board(U, "minus", "after_w")
 
         magnitude(pw_mag[2][:], pw[0][:])
         smaller(hid_rows[:, 2, :], 2, 0, C)
-
-        def weave(lo, hi):
-            woven = sb.tile([P, hi - lo, PACK], BF16, name="hid", tag="hid", bufs=2, align_bytes=64)
+        hid = []
+        for i, (lo, hi) in enumerate(COLUMN_PIECES):
+            woven = sb.tile([P, hi - lo, PACK], BF16, name="hid%d" % i, tag="after_hid%d" % i, align_bytes=64)
             nc.vector.tensor_copy(
                 woven[:, :, 0 : PACK - 1], hid_rows[:, :, lo:hi].rearrange("p t c -> p c t")
             )
-            return woven
-
-        hid = [weave(lo, hi) for lo, hi in COLUMN_PIECES[:2]]
-        magnitude(pw_mag[3][:], pw[1][:])
+            hid.append(woven)
 
         p_vals = [sb.tile([P, C], F32, name="p_vals%d" % nt) for nt in range(2)]
         acc1 = ps.tile([P, C], F32, name="acc1", tag="acc1", bufs=1)
@@ -206,10 +217,10 @@ def tile_picked_tokens_plain_twin_bothlanded_store_divergence_kernel(
             )
 
         for i, (lo, hi) in enumerate(COLUMN_PIECES):
-            if i == len(hid):
-                hid.append(weave(lo, hi))
-            smaller(hid[i][:, :, PACK - 1], PACK - 1, lo, hi)
-            codes = sb.tile([P, hi - lo], U32, name="codes%d" % i, align_bytes=64)
+            last_mag = sb.tile([P, hi - lo], F32, name="last_mag%d" % i, tag="after_hid%d" % (i - 1), align_bytes=64)
+            magnitude(last_mag[:], pw[1][:, lo:hi])
+            nc.vector.tensor_tensor(hid[i][:, :, PACK - 1], last_mag[:], pv[1][:, lo:hi], ALU.min)
+            codes = sb.tile([P, hi - lo], U32, name="codes%d" % i, tag="after_codes%d" % i, align_bytes=64)
             scales = sb.tile([P, hi - lo], U8, name="scales%d" % i, align_bytes=64)
             nc.vector.quantize_mx(
                 out=codes[:].bitcast(FP8X4), scales=scales[:], in_=hid[i][:].rearrange("p c t -> p (c t)")
@@ -225,7 +236,7 @@ def tile_picked_tokens_plain_twin_bothlanded_store_divergence_kernel(
             scatter(minus, l6, lo, hi, p_vals[0][:, lo:hi])
         nc.vector.tensor_copy(p_vals[1][:], acc1[:])
 
-        plus.append(zeroed_board(U, "plus1", "reuse3"))
+        plus.append(zeroed_board(U, "plus1", "after_codes3"))
         page0 = sb.tile([P, U], F32, name="page0")
         nc.vector.tensor_tensor(page0[:], plus[0][:], minus[:], ALU.subtract)
         nc.sync.dma_start(out[0:P, :], page0[:])

@@ -21,7 +21,7 @@ PACK = 4
 QUADS = 4
 STRIPE = 16
 SLOT_PIECES = ((0, 128), (128, J))
-COLUMN_PIECES = tuple((lo, lo + 128) for lo in range(0, C, 128))
+COLUMN_PIECES = ((0, 128), (128, 256), (256, C))
 STORE_PIECES = ((0, 128), (128, 384), (384, 640), (640, 896), (896, U))
 
 
@@ -50,7 +50,7 @@ def tile_picked_tokens_plain_twin_bothlanded_store_divergence_kernel(
 
         def load_scale_rows(scales, name):
             width = scales.shape[2]
-            plane = sb.tile([P, width], U8, name=name, align_bytes=64)
+            plane = sb.tile([P, width], U8, name=name, tag=name, align_bytes=64)
             for q in range(QUADS):
                 rows = scales[0, 4 * q : 4 * q + 4, :].bitcast(I32)
                 nc.sync.dma_start(
@@ -64,8 +64,8 @@ def tile_picked_tokens_plain_twin_bothlanded_store_divergence_kernel(
             nc.vector.memset(board[:], 0.0)
             return board
 
-        def deal_scales(plane, t0, t1, name):
-            dealt = sb.tile([P, t1 - t0, P], U8, name=name, align_bytes=64)
+        def deal_scales(plane, t0, t1, name, tag):
+            dealt = sb.tile([P, t1 - t0, P], U8, name=name, tag=tag, align_bytes=64)
             nc.vector.tensor_copy(dealt[:], plane[:].rearrange("p (m t) -> p t m", t=PACK)[:, t0:t1, :])
             return dealt
 
@@ -82,7 +82,7 @@ def tile_picked_tokens_plain_twin_bothlanded_store_divergence_kernel(
         w_raw = sb.tile([P, R], U32, name="w_raw", tag="after_w", align_bytes=64)
         nc.scalar.dma_start(w_raw[:].bitcast(I32), w_words[0].rearrange("p n t -> p (n t)").bitcast(I32))
         l2 = load_list(offs2, "l2")
-        w2_raw = sb.tile([P, R], I32, name="w2_raw", align_bytes=64)
+        w2_raw = sb.tile([P, R], I32, name="w2_raw", tag="after_w2", align_bytes=64)
         nc.sync.dma_start(w2_raw[:], w2_words[0].rearrange("p n t -> p (n t)").bitcast(I32))
         w2s_plane = load_scale_rows(w2_scales, "w2s_plane")
         l3 = load_list(offs3, "l3")
@@ -92,12 +92,11 @@ def tile_picked_tokens_plain_twin_bothlanded_store_divergence_kernel(
         l4 = load_list(offs4, "l4")
         l5 = load_list(offs5, "l5")
         l6 = load_list(offs6, "l6")
-        pw = [zeroed_board(C, "pw%d" % i, "pw%d" % i) for i in range(2)]
-        pv = [zeroed_board(C, "pv%d" % i, "pv%d" % i) for i in range(2)]
+        pw = [zeroed_board(C, "pw%d" % i, "pw%d" % i) for i in range(3)]
 
         for q in range(QUADS):
             nc.vector.tensor_copy(ws_plane[32 * q : 32 * q + 4, :].bitcast(I32), ws_stage[:, q, :])
-        ws_dealt = [deal_scales(ws_plane, t, t + 1, "ws_dealt%d" % t) for t in range(2)]
+        ws_dealt = [deal_scales(ws_plane, t, t + 1, "ws_dealt%d" % t, "after_ws%d" % t) for t in range(2)]
         w_dealt = []
         for h in range(2):
             dealt = sb.tile([P, 2, P], U32, name="w_dealt%d" % h, align_bytes=64)
@@ -131,12 +130,7 @@ def tile_picked_tokens_plain_twin_bothlanded_store_divergence_kernel(
                     nc.vector.tensor_copy(a_vals[t][:, lo:hi], acc[:])
                 scatter(pw[t], l2, lo, hi, a_vals[t][:, lo:hi])
 
-        w2_dealt = sb.tile([P, PACK, P], I32, name="w2_dealt", align_bytes=64)
-        nc.vector.tensor_copy(
-            w2_dealt[:].rearrange("p t m -> p m t"), w2_raw[:].rearrange("p (m t) -> p m t", t=PACK)
-        )
-        w2s_dealt = deal_scales(w2s_plane, 0, PACK, "w2s_dealt")
-        ws_dealt.append(deal_scales(ws_plane, 2, PACK, "ws_dealt2"))
+        ws_dealt.append(deal_scales(ws_plane, 2, PACK, "ws_dealt2", "ws_dealt2"))
 
         def whole_product(words, scales):
             acc = ps.tile([P, J], F32, name="whole", tag="whole", bufs=3)
@@ -159,19 +153,25 @@ def tile_picked_tokens_plain_twin_bothlanded_store_divergence_kernel(
             magnitude(b_mag[:], b_vals[:])
             return b_mag
 
-        b_mags = [make_b(0), make_b(1)]
-        for t in (2, 3):
-            make_a(t)
-            b_mags.append(make_b(t))
+        make_a(2)
+        w2_dealt = sb.tile([P, PACK, P], I32, name="w2_dealt", tag="after_ws1", align_bytes=64)
+        nc.vector.tensor_copy(
+            w2_dealt[:].rearrange("p t m -> p m t"), w2_raw[:].rearrange("p (m t) -> p m t", t=PACK)
+        )
+        w2s_dealt = deal_scales(w2s_plane, 0, PACK, "w2s_dealt", "after_ws0")
+        pv = [zeroed_board(C, "pv0", "after_w2"), zeroed_board(C, "pv1", "w2s_plane")]
+        b_mags = [make_b(t) for t in range(3)]
+        make_a(3)
+        b_mags.append(make_b(3))
 
         def land_a(t):
-            scatter(pw[t % 2], l2, 0, J, a_vals[t][:])
+            scatter(pw[t % 3], l2, 0, J, a_vals[t][:])
 
         def land_b(t):
             scatter(pv[t % 2], l3, 0, J, b_mags[t][:])
 
         pw_mag = [
-            sb.tile([P, C], F32, name="pw_mag%d" % t, tag="after_b%d" % t if t < 2 else "pw_mag%d" % t, align_bytes=64)
+            sb.tile([P, C], F32, name="pw_mag%d" % t, tag="after_b%d" % t, align_bytes=64)
             for t in range(PACK - 1)
         ]
         hid_rows = sb.tile([P, PACK - 1, C], BF16, name="hid_rows")
@@ -179,25 +179,24 @@ def tile_picked_tokens_plain_twin_bothlanded_store_divergence_kernel(
         def smaller(dst, t, lo, hi):
             nc.vector.tensor_tensor(dst, pw_mag[t][:, lo:hi], pv[t % 2][:, lo:hi], ALU.min)
 
+        land_a(2)
         land_b(0)
         land_b(1)
-        magnitude(pw_mag[0][:], pw[0][:])
-        magnitude(pw_mag[1][:], pw[1][:])
-        land_a(2)
+        for t in range(3):
+            magnitude(pw_mag[t][:], pw[t][:])
         smaller(hid_rows[:, 0, :], 0, 0, C)
         land_b(2)
         land_a(3)
         smaller(hid_rows[:, 1, :], 1, 0, C)
         land_b(3)
 
-        vw = sb.tile([P, N], U16, name="vw", tag="after_b2", align_bytes=64)
-        vsc = sb.tile([P, N], U8, name="vsc", tag="after_b3", align_bytes=64)
+        vw = sb.tile([P, N], U16, name="vw", tag="after_b3", align_bytes=64)
+        vsc = sb.tile([P, N], U8, name="vsc", tag="after_ws0", align_bytes=64)
         nc.vector.tensor_copy(vw[:], vw_win[:].indirect(l4[:]))
         nc.vector.tensor_copy(vsc[:], vss_win[:].indirect(l4[:]))
         plus = [zeroed_board(U, "plus0", "xs_rest")]
         minus = zeroed_board(U, "minus", "after_w")
 
-        magnitude(pw_mag[2][:], pw[0][:])
         smaller(hid_rows[:, 2, :], 2, 0, C)
         hid = []
         for i, (lo, hi) in enumerate(COLUMN_PIECES):
@@ -217,8 +216,8 @@ def tile_picked_tokens_plain_twin_bothlanded_store_divergence_kernel(
             )
 
         for i, (lo, hi) in enumerate(COLUMN_PIECES):
-            last_mag = sb.tile([P, hi - lo], F32, name="last_mag%d" % i, tag="after_hid%d" % (i - 1), align_bytes=64)
-            magnitude(last_mag[:], pw[1][:, lo:hi])
+            last_mag = sb.tile([P, hi - lo], F32, name="last_mag%d" % i, tag="after_hid%d" % (i - 2), align_bytes=64)
+            magnitude(last_mag[:], pw[0][:, lo:hi])
             nc.vector.tensor_tensor(hid[i][:, :, PACK - 1], last_mag[:], pv[1][:, lo:hi], ALU.min)
             codes = sb.tile([P, hi - lo], U32, name="codes%d" % i, tag="after_codes%d" % i, align_bytes=64)
             scales = sb.tile([P, hi - lo], U8, name="scales%d" % i, align_bytes=64)
@@ -236,7 +235,7 @@ def tile_picked_tokens_plain_twin_bothlanded_store_divergence_kernel(
             scatter(minus, l6, lo, hi, p_vals[0][:, lo:hi])
         nc.vector.tensor_copy(p_vals[1][:], acc1[:])
 
-        plus.append(zeroed_board(U, "plus1", "after_codes3"))
+        plus.append(zeroed_board(U, "plus1", "after_codes2"))
         page0 = sb.tile([P, U], F32, name="page0")
         nc.vector.tensor_tensor(page0[:], plus[0][:], minus[:], ALU.subtract)
         nc.sync.dma_start(out[0:P, :], page0[:])

from contextlib import ExitStack

import concourse.mybir as mybir

K, J, R, T, C, N, S, U = 512, 384, 512, 1024, 512, 256, 1024, 1024
FLOPS = 2 * (2 * K * R * J + R * N * C)

F32 = mybir.dt.float32
BF16 = mybir.dt.bfloat16
I32 = mybir.dt.int32
U32 = mybir.dt.uint32
U16 = mybir.dt.uint16
U8 = mybir.dt.uint8
FP8X4 = mybir.dt.float8_e4m3fn_x4
FP4X4 = mybir.dt.float4_e2m1fn_x4
ALU = mybir.AluOpType
COPY = mybir.ActivationFunctionType.Copy

P = 128
PACK = 4
QUADS = 4
STRIPE = 16
SLOT_PIECES = ((0, 128), (128, J))
COLUMN_PIECES = ((0, 128), (128, 256), (256, C))
STORE_PIECES = ((0, 128), (128, 384), (384, 640), (640, 896), (896, U))


def tile_picked_tokens_plain_twin_bothlanded_store_divergence_kernel(
    tc, xt_words, xt_scales, w_words, w_scales, w2_words, w2_scales, vs_words, vs_scales,
    offs, offs2, offs3, offs4, offs5, offs6, out,
):
    nc = tc.nc
    with ExitStack() as ctx:
        lists = ctx.enter_context(tc.tile_pool(name="lists", bufs=1))
        sb = ctx.enter_context(tc.tile_pool(name="sb", bufs=1))
        ps = ctx.enter_context(tc.psum_pool(name="ps", bufs=1))

        def load_list(src, name):
            held = lists.tile(list(src.shape), U16, name=name)
            nc.sync.dma_start(held[:], src)
            return held

        def entries(held, lo, hi):
            return held[:, lo // STRIPE : hi // STRIPE]

        def zeroed_plane(width, name):
            plane = sb.tile([P, width], U8, name=name, align_bytes=64)
            nc.vector.memset(plane[:].bitcast(I32), 0)
            return plane

        def load_scale_rows(scales, name):
            width = scales.shape[2]
            plane = sb.tile([P, width], U8, name=name, tag=name, align_bytes=64)
            for q in range(QUADS):
                rows = scales[0, 4 * q : 4 * q + 4, :].bitcast(I32)
                nc.sync.dma_start(
                    plane[32 * q : 32 * q + 32, :].bitcast(I32),
                    rows.unsqueeze(0).broadcast_to([8, 4, width // 4]),
                )
            return plane

        def zeroed_board(width, name, tag):
            board = sb.tile([P, width], F32, name=name, tag=tag, align_bytes=64)
            nc.vector.memset(board[:], 0.0)
            return board

        def deal_scales(plane, t0, t1, name, tag):
            dealt = sb.tile([P, t1 - t0, P], U8, name=name, tag=tag, align_bytes=64)
            nc.vector.tensor_copy(dealt[:], plane[:].rearrange("p (m t) -> p t m", t=PACK)[:, t0:t1, :])
            return dealt

        def scatter(board, held, lo, hi, values):
            nc.scalar.activation(out=board[:].indirect(entries(held, lo, hi)), in_=values, func=COPY)

        ws_plane = zeroed_plane(R, "ws_plane")
        l1 = load_list(offs, "l1")
        xw_win = sb.tile([P, T], U16, name="xw_win", align_bytes=64)
        xs_win = load_scale_rows(xt_scales, "xs_win")
        ws_stage = sb.tile([4, QUADS, R // 4], I32, name="ws_stage")
        nc.scalar.dma_start(ws_stage[:], w_scales[0].bitcast(I32).rearrange("(q i) c -> i q c", i=4))
        nc.scalar.dma_start(xw_win[:].bitcast(I32), xt_words[0].bitcast(I32))
        w_raw = sb.tile([P, R], U32, name="w_raw", tag="after_w", align_bytes=64)
        nc.scalar.dma_start(w_raw[:].bitcast(I32), w_words[0].rearrange("p n t -> p (n t)").bitcast(I32))
        l2 = load_list(offs2, "l2")
        w2_raw = sb.tile([P, R], I32, name="w2_raw", tag="after_w2", align_bytes=64)
        nc.sync.dma_start(w2_raw[:], w2_words[0].rearrange("p n t -> p (n t)").bitcast(I32))
        w2s_plane = load_scale_rows(w2_scales, "w2s_plane")
        l3 = load_list(offs3, "l3")
        vw_win = sb.tile([P, S], U16, name="vw_win", align_bytes=64)
        nc.sync.dma_start(vw_win[:].bitcast(I32), vs_words[0].bitcast(I32))
        vss_win = load_scale_rows(vs_scales, "vss_win")
        l4 = load_list(offs4, "l4")
        l5 = load_list(offs5, "l5")
        l6 = load_list(offs6, "l6")
        pw = [zeroed_board(C, "pw%d" % i, "pw%d" % i) for i in range(3)]

        for q in range(QUADS):
            nc.vector.tensor_copy(ws_plane[32 * q : 32 * q + 4, :].bitcast(I32), ws_stage[:, q, :])
        ws_dealt = [deal_scales(ws_plane, t, t + 1, "ws_dealt%d" % t, "after_ws%d" % t) for t in range(2)]
        w_dealt = []
        for h in range(2):
            dealt = sb.tile([P, 2, P], U32, name="w_dealt%d" % h, align_bytes=64)
            nc.scalar.copy(
                dealt[:].rearrange("p t m -> p m t"),
                w_raw[:].rearrange("p (m t) -> p m t", t=PACK)[:, :, 2 * h : 2 * h + 2],
            )
            w_dealt.append(dealt)

        xw, xs = {}, {}
        for (lo, hi), word_tag, scale_tag in zip(SLOT_PIECES, ("xw_first", "after_w"), ("xs_first", "xs_rest")):
            xw[lo] = sb.tile([P, hi - lo], U16, name="xw%d" % lo, tag=word_tag, align_bytes=64)
            xs[lo] = sb.tile([P, hi - lo], U8, name="xs%d" % lo, tag=scale_tag, align_bytes=64)
            nc.vector.tensor_copy(xw[lo][:], xw_win[:].indirect(entries(l1, lo, hi)))
            nc.vector.tensor_copy(xs[lo][:], xs_win[:].indirect(entries(l1, lo, hi)))

        def first_product(acc, words, scales, lo, hi):
            nc.tensor.matmul_mx(
                out=acc, lhsT=words.bitcast(FP8X4), lhsT_scale=scales,
                rhs=xw[lo][:].bitcast(FP4X4), rhs_scale=xs[lo][:], start=True, stop=True,
            )

        a_vals = [sb.tile([P, J], F32, name="a_vals%d" % t) for t in range(PACK)]
        for lo, hi in SLOT_PIECES:
            for t in range(2):
                acc = ps.tile([P, hi - lo], F32, name="piece", tag="piece", bufs=4)
                first_product(acc[:], w_dealt[0][:, t, :], ws_dealt[t][:, 0, :], lo, hi)
                if lo == 0 and t == 0:
                    nc.scalar.activation(out=a_vals[t][:, lo:hi], in_=acc[:], func=COPY)
                else:
                    nc.vector.tensor_copy(a_vals[t][:, lo:hi], acc[:])
                scatter(pw[t], l2, lo, hi, a_vals[t][:, lo:hi])

        ws_dealt.append(deal_scales(ws_plane, 2, PACK, "ws_dealt2", "ws_dealt2"))

        def whole_product(words, scales):
            acc = ps.tile([P, J], F32, name="whole", tag="whole", bufs=3)
            for lo, hi in SLOT_PIECES:
                first_product(acc[:, lo:hi], words, scales, lo, hi)
            return acc

        def magnitude(dst, src):
            nc.vector.scalar_tensor_tensor(out=dst, in0=src, scalar=-1.0, in1=src, op0=ALU.mult, op1=ALU.max)

        def make_a(t):
            acc = whole_product(w_dealt[1][:, t - 2, :], ws_dealt[2][:, t - 2, :])
            nc.vector.tensor_copy(a_vals[t][:], acc[:])

        def make_b(t):
            acc = whole_product(w2_dealt[:, t, :], w2s_dealt[:, t, :])
            b_vals = sb.tile([P, J], F32, name="b_vals%d" % t, tag="after_b%d" % t, align_bytes=64)
            nc.vector.tensor_copy(b_vals[:], acc[:])
            b_mag = sb.tile([P, J], F32, name="b_mag%d" % t)
            magnitude(b_mag[:], b_vals[:])
            return b_mag

        make_a(2)
        w2_dealt = sb.tile([P, PACK, P], I32, name="w2_dealt", tag="after_ws1", align_bytes=64)
        nc.vector.tensor_copy(
            w2_dealt[:].rearrange("p t m -> p m t"), w2_raw[:].rearrange("p (m t) -> p m t", t=PACK)
        )
        w2s_dealt = deal_scales(w2s_plane, 0, PACK, "w2s_dealt", "after_ws0")
        pv = [zeroed_board(C, "pv0", "after_w2"), zeroed_board(C, "pv1", "w2s_plane")]
        b_mags = [make_b(t) for t in range(3)]
        make_a(3)
        b_mags.append(make_b(3))

        def land_a(t):
            scatter(pw[t % 3], l2, 0, J, a_vals[t][:])

        def land_b(t):
            scatter(pv[t % 2], l3, 0, J, b_mags[t][:])

        pw_mag = [
            sb.tile([P, C], F32, name="pw_mag%d" % t, tag="after_b%d" % t, align_bytes=64)
            for t in range(PACK - 1)
        ]
        hid_rows = sb.tile([P, PACK - 1, C], BF16, name="hid_rows")

        def smaller(dst, t, lo, hi):
            nc.vector.tensor_tensor(dst, pw_mag[t][:, lo:hi], pv[t % 2][:, lo:hi], ALU.min)

        land_a(2)
        land_b(0)
        land_b(1)
        for t in range(3):
            magnitude(pw_mag[t][:], pw[t][:])
        smaller(hid_rows[:, 0, :], 0, 0, C)
        land_b(2)
        land_a(3)
        smaller(hid_rows[:, 1, :], 1, 0, C)
        land_b(3)

        vw = sb.tile([P, N], U16, name="vw", tag="after_b3", align_bytes=64)
        vsc = sb.tile([P, N], U8, name="vsc", tag="after_ws0", align_bytes=64)
        nc.vector.tensor_copy(vw[:], vw_win[:].indirect(l4[:]))
        nc.vector.tensor_copy(vsc[:], vss_win[:].indirect(l4[:]))
        plus = [zeroed_board(U, "plus0", "xs_rest")]
        minus = zeroed_board(U, "minus", "after_w")

        smaller(hid_rows[:, 2, :], 2, 0, C)
        hid = []
        for i, (lo, hi) in enumerate(COLUMN_PIECES):
            woven = sb.tile([P, hi - lo, PACK], BF16, name="hid%d" % i, tag="after_hid%d" % i, align_bytes=64)
            nc.vector.tensor_copy(
                woven[:, :, 0 : PACK - 1], hid_rows[:, :, lo:hi].rearrange("p t c -> p c t")
            )
            hid.append(woven)

        p_vals = [sb.tile([P, C], F32, name="p_vals%d" % nt) for nt in range(2)]
        acc1 = ps.tile([P, C], F32, name="acc1", tag="acc1", bufs=1)

        def second_product(acc, nt, codes, scales):
            nc.tensor.matmul_mx(
                out=acc, lhsT=vw[:, nt * P : (nt + 1) * P].bitcast(FP4X4), lhsT_scale=vsc[:, nt * P : (nt + 1) * P],
                rhs=codes[:].bitcast(FP8X4), rhs_scale=scales[:], start=True, stop=True,
            )

        for i, (lo, hi) in enumerate(COLUMN_PIECES):
            last_mag = sb.tile([P, hi - lo], F32, name="last_mag%d" % i, tag="after_hid%d" % (i - 2), align_bytes=64)
            magnitude(last_mag[:], pw[0][:, lo:hi])
            nc.vector.tensor_tensor(hid[i][:, :, PACK - 1], last_mag[:], pv[1][:, lo:hi], ALU.min)
            codes = sb.tile([P, hi - lo], U32, name="codes%d" % i, tag="after_codes%d" % i, align_bytes=64)
            scales = sb.tile([P, hi - lo], U8, name="scales%d" % i, align_bytes=64)
            nc.vector.quantize_mx(
                out=codes[:].bitcast(FP8X4), scales=scales[:], in_=hid[i][:].rearrange("p c t -> p (c t)")
            )
            acc = ps.tile([P, hi - lo], F32, name="piece", tag="piece", bufs=4)
            second_product(acc[:], 0, codes, scales)
            second_product(acc1[:, lo:hi], 1, codes, scales)
            if i == 0:
                nc.scalar.copy(p_vals[0][:, lo:hi], acc[:])
            else:
                nc.vector.tensor_copy(p_vals[0][:, lo:hi], acc[:])
            scatter(plus[0], l5, lo, hi, p_vals[0][:, lo:hi])
            scatter(minus, l6, lo, hi, p_vals[0][:, lo:hi])
        nc.vector.tensor_copy(p_vals[1][:], acc1[:])

        plus.append(zeroed_board(U, "plus1", "after_codes2"))
        page0 = sb.tile([P, U], F32, name="page0")
        nc.vector.tensor_tensor(page0[:], plus[0][:], minus[:], ALU.subtract)
        nc.sync.dma_start(out[0:P, :], page0[:])
        scatter(plus[1], l5, 0, C, p_vals[1][:])
        scatter(minus, l6, 0, C, p_vals[1][:])
        for i, (lo, hi) in enumerate(STORE_PIECES):
            page = sb.tile([P, hi - lo], F32, name="page1_%d" % i)
            nc.vector.tensor_tensor(page[:], plus[1][:, lo:hi], minus[:, lo:hi], ALU.subtract)
            nc.sync.dma_start(out[P : 2 * P, lo:hi], page[:])
